import numpy as np
import ml_dtypes


def mxq(x, axis, fmt="e4m3"):
    dtype, down = {"e4m3": (ml_dtypes.float8_e4m3fn, 7), "e5m2": (ml_dtypes.float8_e5m2, 14)}[fmt]
    v = np.moveaxis(np.asarray(x, np.float32).astype(ml_dtypes.bfloat16).astype(np.float64), axis, -1)
    blocks = v.reshape(v.shape[:-1] + (-1, 32))
    amax = np.abs(blocks).max(-1, keepdims=True)
    byte = np.maximum(np.where(amax > 0, np.frexp(amax)[1] - 1 + 127, 0) - down, 1)
    scale = np.exp2(byte - 127.0)
    codes = (blocks / scale).astype(np.float32).astype(dtype).astype(np.float64)
    return np.moveaxis((codes * scale).reshape(v.shape), -1, axis)


WIDE = False


def mx_kscale(k):
    if not WIDE:
        return np.ones(k)
    levels = np.array([10, -10, 5, -5, 0])
    if k % 512:
        return np.exp2(np.random.permutation(np.resize(levels, k // 32))).repeat(32)
    a = np.empty((k // 512, 16))
    for p in range(k // 512):
        a[p, :8] = np.random.permutation(np.resize(levels, 8))
        for g in range(8):
            far = levels[np.abs(levels - a[p, g]) >= 10]
            a[p, g + 8] = far[np.random.randint(len(far))]
    return np.exp2(a.ravel()).repeat(32)


def f64(x):
    return np.asarray(x).astype(np.float64)


def striped(idx):
    return np.tile(idx.reshape(-1, 16).T, (8, 1)).astype(np.uint16)


def unstriped(offs):
    return offs[:16].T.reshape(-1).astype(np.int64)


def pack_weight(w):
    k, n = w.shape
    w = f64(np.asarray(w, np.float32).astype(ml_dtypes.bfloat16)).reshape(k // 32, 32, n)
    amax = np.abs(w).max(1)
    byte = np.clip(np.where(amax > 0, np.frexp(amax)[1] - 1 + 127 - 7, 1), 1, 254)
    scaled = (w * np.exp2(127.0 - byte)[:, None, :]).reshape(k, n).astype(np.float32)
    words = np.ascontiguousarray(scaled.reshape(k // 512, 128, 4, n).transpose(0, 1, 3, 2)).astype(ml_dtypes.float8_e4m3fn).view(np.uint8)
    return words, np.ascontiguousarray(byte.astype(np.uint8).reshape(k // 512, 16, n))


def unpack_weight(words, scales):
    g, p, n, _ = words.shape
    vals = np.ascontiguousarray(words).view(ml_dtypes.float8_e4m3fn).astype(np.float64) * np.repeat(np.exp2(scales.astype(np.float64) - 127.0), 8, axis=1)[..., None]
    return vals.transpose(0, 1, 3, 2).reshape(g * 512, n)


E2M1 = np.array([0.0, 0.5, 1.0, 1.5, 2.0, 3.0, 4.0, 6.0, -0.0, -0.5, -1.0, -1.5, -2.0, -3.0, -4.0, -6.0])


def pack_fp4(w):
    k, n = w.shape
    w = f64(np.asarray(w, np.float32).astype(ml_dtypes.bfloat16)).reshape(k // 32, 32, n)
    amax = np.abs(w).max(1)
    mant, ex = np.frexp(amax / 6.0)
    byte = np.clip(np.where(amax > 0, np.where(mant > 0.5, ex, ex - 1) + 127, 1), 1, 254)
    scaled = (w * np.exp2(127.0 - byte)[:, None, :]).reshape(k, n).astype(np.float32)
    c = np.ascontiguousarray(scaled.reshape(k // 512, 128, 4, n).transpose(0, 1, 3, 2)).astype(ml_dtypes.float4_e2m1fn).view(np.uint8) & 0xF
    words = (c[..., 0::2] | (c[..., 1::2] << 4)).reshape(k // 512, 128, 2 * n)
    return np.ascontiguousarray(words), np.ascontiguousarray(byte.astype(np.uint8).reshape(k // 512, 16, n))


def unpack_fp4(words, scales):
    g, _, n = scales.shape
    words = np.ascontiguousarray(words).reshape(g, 128, n, 2)
    nib = np.empty((g, 128, n, 4), np.uint8)
    nib[..., 0::2] = words & 0xF
    nib[..., 1::2] = words >> 4
    vals = E2M1[nib] * np.repeat(np.exp2(scales.astype(np.float64) - 127.0), 8, axis=1)[..., None]
    return vals.transpose(0, 1, 3, 2).reshape(g * 512, n)


def sigmoid(v):
    return 1.0 / (1.0 + np.exp(-np.maximum(v, -700.0)))

def planes(y):
    n, m = y.shape
    v = y.astype(np.float32).astype(ml_dtypes.bfloat16).astype(np.float64).reshape(n // 32, 32, m)
    top = np.abs(v).max(1)
    byte = np.clip(np.where(top > 0, np.frexp(top)[1] - 1 + 127 - 7, 1), 1, 254)
    codes = (v * np.exp2(127.0 - byte)[:, None, :]).reshape(n, m).astype(np.float32).astype(ml_dtypes.float8_e4m3fn).view(np.uint8)
    words = codes.reshape(n // 512, 128, 4, m).transpose(0, 1, 3, 2)
    return np.ascontiguousarray(words), np.ascontiguousarray(byte.astype(np.uint8).reshape(n // 512, 16, m))


K, T, S, N, H, W = 512, 2048, 512, 512, 512, 2048


def setup_inputs():
    n = np.random.standard_normal
    s = mx_kscale(K)[:, None]
    u = mx_kscale(H)
    packed_xT = pack_weight(n((K, T)) * s)
    packed_w1 = pack_fp4(n((K, H)) / np.sqrt(K) / s)
    packed_w2 = pack_fp4(n((H, N)) / np.sqrt(2 * H) / u[:, None])
    packed_w3 = pack_fp4(n((K, N)) / np.sqrt(2 * K) / s)
    return {
        "x_words": packed_xT[0],
        "x_scales": packed_xT[1],
        "w1_words": packed_w1[0],
        "w1_scales": packed_w1[1],
        "gn": (np.random.uniform(0.5, 1.5, (H, 1)) * u[:, None]).astype(np.float32),
        "w2_words": packed_w2[0],
        "w2_scales": packed_w2[1],
        "w3_words": packed_w3[0],
        "w3_scales": packed_w3[1],
        "offs": striped(np.random.permutation(T)[:S]),
        "n1": striped(np.random.randint(0, S, W)),
        "two": striped(np.random.permutation(T)[:S]),
        "n2": striped(np.random.permutation(S)),
        "n3": striped(np.random.permutation(S)),
        "n4": striped(np.random.permutation(S)),
    }


def reference(x_words, x_scales, w1_words, w1_scales, gn, w2_words, w2_scales, w3_words, w3_scales, offs, n1, two, n2, n3, n4):
    xq = unpack_weight(x_words, x_scales)[:, unstriped(offs)]
    y = unpack_fp4(w1_words, w1_scales).T @ xq
    mb = y[:, unstriped(n1)]
    ms = mb.reshape(H, S, 4).sum(axis=2)
    z = f64(gn) * (y * sigmoid(ms))
    x_two = unpack_weight(x_words, x_scales)[:, unstriped(two)]
    h = unpack_fp4(w2_words, w2_scales).T @ mxq(z, 0, "e4m3") + unpack_fp4(w3_words, w3_scales).T @ x_two
    st = h - h[:, unstriped(n2)]
    su = np.maximum(st, st[:, unstriped(n3)])
    out_0 = su + 0.5 * su[:, unstriped(n4)]
    return (out_0,) + planes(out_0)

@@ -1,0 +1,340 @@
+from contextlib import ExitStack
+
+import concourse.mybir as mybir
+from concourse.masks import make_identity
+
+F32 = mybir.dt.float32
+BF16 = mybir.dt.bfloat16
+I32 = mybir.dt.int32
+U32 = mybir.dt.uint32
+U16 = mybir.dt.uint16
+U8 = mybir.dt.uint8
+FP8X4 = mybir.dt.float8_e4m3fn_x4
+FP4X4 = mybir.dt.float4_e2m1fn_x4
+ALU = mybir.AluOpType
+ACT = mybir.ActivationFunctionType
+
+P = 128
+PACK = 4
+T = 2048
+S = 512
+MEMBERS = 4
+BLOCK = 128
+BLOCKS = S // BLOCK
+HALF = S // 2
+SPARE = 8
+PER_COL = 16
+
+IL_SCALAR = (True, True)
+G3_A = 2
+G3_B = 3
+G2_EARLY = 4
+LEFT_SCALAR = ()
+C_VECTOR = ((3, 0),)
+IL_OUT = (True, False)
+SUB_POOL = ()
+WARM = False
+B3 = (False, False)
+
+FLOPS = 3 * 2 * 512 * 512 * 512
+
+
+def tile_picked_mixingsumgthree_none_po_kernel(
+    tc, x_words, x_scales, w1_words, w1_scales, gn, w2_words, w2_scales, w3_words, w3_scales,
+    offs, n1, two, n2, n3, n4, out_0, out_1, out_2,
+):
+    nc = tc.nc
+    with ExitStack() as ctx:
+        lists = ctx.enter_context(tc.tile_pool(name="lists", bufs=1))
+        keep = ctx.enter_context(tc.tile_pool(name="keep", bufs=1))
+        ring = ctx.enter_context(tc.tile_pool(name="ring", bufs=2))
+        psum = ctx.enter_context(tc.psum_pool(name="psum", bufs=1))
+
+        def load_list(name, src):
+            tile = lists.tile([P, src.shape[1]], U16, name=name)
+            nc.sync.dma_start(tile[:], src)
+            return tile
+
+        def load_scale_rows(queues, tile, src):
+            for q in range(4):
+                queues[q].dma_start(tile[32 * q : 32 * q + 4].bitcast(I32), src[0, 4 * q : 4 * q + 4, :].bitcast(I32))
+
+        def entries(tile, first, count):
+            return tile[:, first // PER_COL : (first + count) // PER_COL]
+
+        def window(name):
+            tile = keep.tile([P, S + SPARE], F32, name=name)
+            nc.gpsimd.memset(tile[:, S:], 0.0)
+            return tile
+
+        def gather(on_scalar, out, win, offsets):
+            if on_scalar:
+                nc.scalar.activation(out, win[:].indirect(offsets), ACT.Copy)
+            else:
+                nc.vector.tensor_copy(out, win[:].indirect(offsets))
+
+        def interleave(on_scalar, dst, src):
+            copy = nc.scalar.copy if on_scalar else nc.vector.tensor_copy
+            copy(dst.rearrange("p (c i) t -> p c t i", i=4), src.rearrange("p t (c i) -> p c t i", i=4))
+
+        xw = keep.tile([P, T], I32, name="xw")
+        xs = keep.tile([P, T], U8, name="xs")
+        raw_w1 = keep.tile([P, 2 * S], U8, name="raw_w1")
+        raw_w23 = keep.tile([P, 2, 2 * S], U8, name="raw_w23")
+        raw_s23 = keep.tile([P, 2, S], U8, name="raw_s23")
+        raw_s1 = raw_w23[:].rearrange("p i n -> p (i n)")[:, 2 * S - S // 2 : 2 * S + S // 2]
+        nc.vector.memset(xs[:].bitcast(I32), 0)
+        nc.vector.memset(raw_s1.bitcast(I32), 0)
+        nc.vector.memset(raw_s23[:].rearrange("p i n -> p (i n)").bitcast(I32), 0)
+
+        def load_words(queue, tile, words):
+            queue.dma_start(tile.bitcast(I32), words[0].bitcast(I32))
+
+        def deal_words(name, raw):
+            words = keep.tile([P, PACK, P, 2], U8, name=name + "_words", align_bytes=64)
+            nc.gpsimd.tensor_copy(words[:], raw.rearrange("p (m t b) -> p t m b", t=PACK, b=2))
+            return words
+
+        def deal_scales(name, raw):
+            scales = keep.tile([P, PACK, P], U8, name=name + "_scales", align_bytes=64)
+            nc.gpsimd.tensor_copy(scales[:], raw.rearrange("p (m t) -> p t m", t=PACK))
+            return scales
+
+        def pick(name, offsets, pieces):
+            scales = keep.tile([P, S], U8, name=name + "_scales", align_bytes=64)
+            words = keep.tile([P, S], U32, name=name + "_words", align_bytes=64)
+            nc.vector.tensor_copy(scales[:], xs[:].indirect(offsets[:]))
+            for u in range(pieces):
+                n = S // pieces
+                nc.vector.tensor_copy(words[:, u * n : (u + 1) * n], xw[:].bitcast(U32).indirect(entries(offsets, u * n, n)))
+            return words, scales
+
+        def product(out, weight, t, words, scales, start, stop):
+            nc.tensor.matmul_mx(
+                out,
+                lhsT=weight[0][:, t, :, :].rearrange("p m b -> p (m b)").bitcast(FP4X4),
+                lhsT_scale=weight[1][:, t, :],
+                rhs=words.bitcast(FP8X4),
+                rhs_scale=scales,
+                start=start,
+                stop=stop,
+            )
+
+        offs_t = load_list("offs_t", offs)
+        load_words(nc.scalar, raw_w1[:], w1_words)
+        two_t = load_list("two_t", two)
+        load_scale_rows([nc.scalar, nc.scalar, nc.sync, nc.sync], xs[:], x_scales)
+        nc.scalar.dma_start(xw[:], x_words[0].rearrange("p n t -> p (n t)").bitcast(I32))
+        load_scale_rows([nc.sync] * 4, raw_s1, w1_scales)
+        n1_t = load_list("n1_t", n1)
+        load_scale_rows([nc.sync] * 4, raw_s23[:, 0, :], w3_scales)
+        load_scale_rows([nc.sync] * 4, raw_s23[:, 1, :], w2_scales)
+        gain = keep.tile([P, PACK], F32, name="gain")
+        nc.sync.dma_start(gain[:], gn.rearrange("(p t) o -> p (t o)", t=PACK))
+        n2_t = load_list("n2_t", n2)
+        n3_t = load_list("n3_t", n3)
+        n4_t = load_list("n4_t", n4)
+
+        y = [window("y%d" % t) for t in range(PACK)]
+        h = [window("h%d" % t) for t in range(PACK)]
+        neg_st = [window("neg_st%d" % t) for t in range(PACK)]
+        neg_su = [keep.tile([P, S], F32, name="neg_su%d" % t) for t in range(PACK)]
+
+        if WARM:
+            warm = keep.tile([P, SPARE], F32, name="warm")
+            nc.scalar.activation(warm[:], y[0][:, S:], ACT.Sigmoid)
+        ident = keep.tile([P, P], F32, name="ident")
+        make_identity(nc, ident[:])
+
+        w1 = (deal_words("w1", raw_w1[:]), deal_scales("w1", raw_s1))
+        load_words(nc.sync, raw_w23[:, 0, :], w3_words)
+        load_words(nc.sync, raw_w23[:, 1, :], w2_words)
+        x1_words, x1_scales = pick("x1", offs_t, 2)
+        y_banks = [psum.tile([P, S], F32, name="bank_a%d" % t) for t in range(PACK)]
+        for t in range(PACK):
+            for u in range(2):
+                cols = slice(u * HALF, (u + 1) * HALF)
+                product(y_banks[t][:, cols], w1, t, x1_words[:, cols], x1_scales[:, cols], True, True)
+            nc.scalar.activation(y[t][:, :S], y_banks[t][:], ACT.Copy)
+
+        x2_words, x2_scales = pick("x2", two_t, 1)
+        w3 = (deal_words("w3", raw_w23[:, 0, :]), deal_scales("w3", raw_s23[:, 0, :]))
+        w2 = (deal_words("w2", raw_w23[:, 1, :]), deal_scales("w2", raw_s23[:, 1, :]))
+
+        h_left = [psum.tile([P, HALF], F32, name="bank_b%d" % t) for t in range(PACK)]
+        z_left = keep.tile([P, PACK, HALF], BF16, name="z_left")
+
+        def look_up_left(t):
+            mb = ring.tile([P, HALF * MEMBERS], F32, name="mb_left", bufs=PACK)
+            for u in range(2):
+                if (t, u) not in LEFT_SCALAR:
+                    gather(False, mb[:, u * S : (u + 1) * S], y[t], entries(n1_t, u * S, S))
+            return mb
+
+        def sum_left(bank, ts):
+            sums = psum.tile([P, S], F32, name="bank_a%d" % bank)
+            for c in range(2 * len(ts)):
+                members = mb_left[ts[c // 2]][:, (c % 2) * S : (c % 2 + 1) * S]
+                for d in range(MEMBERS):
+                    nc.tensor.matmul(
+                        sums[:, c * P : (c + 1) * P], lhsT=members[:, d::MEMBERS], rhs=ident[:],
+                        is_transpose=True, start=d == 0, stop=d == MEMBERS - 1,
+                    )
+            return sums
+
+        def gate_left(bank, ts, sums):
+            n = HALF * len(ts)
+            back = psum.tile([P, S], F32, name="bank_a%d" % bank)
+            turned = ring.tile([P, S], F32, name="turned", bufs=3)
+            nc.scalar.activation(turned[:, :n], sums[:, :n], ACT.Sigmoid)
+            for c in range(2 * len(ts)):
+                nc.tensor.transpose(back[:, c * P : (c + 1) * P], turned[:, c * P : (c + 1) * P], ident[:])
+            return back
+
+        def z_rows_of(dst, sig, t, cols):
+            nc.vector.scalar_tensor_tensor(dst, sig, gain[:, t : t + 1], y[t][:, cols], ALU.mult, ALU.mult)
+
+        def rows_left(ts, back):
+            for i, t in enumerate(ts):
+                z_rows_of(z_left[:, t, :], back[:, i * HALF : (i + 1) * HALF], t, slice(0, HALF))
+
+        def look_up(b, ts, mb):
+            for t in ts:
+                gather(True, mb[:, t, :], y[t], entries(n1_t, b * BLOCK * MEMBERS, BLOCK * MEMBERS))
+
+        def add_members(mb, ts):
+            n = (ts.stop - ts.start) * BLOCK
+            pairs = ring.tile([P, n, 2], F32, name="pairs", bufs=3)
+            ms = ring.tile([P, n], F32, name="ms", bufs=3)
+            members = mb[:, ts, :].rearrange("p t (j d) -> p (t j) d", d=MEMBERS)
+            nc.vector.tensor_tensor(pairs[:], members[:, :, 0:2], members[:, :, 2:4], ALU.add)
+            nc.vector.tensor_tensor(ms[:], pairs[:, :, 0], pairs[:, :, 1], ALU.add)
+            return ms
+
+        def gate(ms, sig, ts):
+            nc.scalar.activation(sig[:, ts, :].rearrange("p t j -> p (t j)"), ms[:], ACT.Sigmoid)
+
+        def rows_right(b, sig, ts, z_rows):
+            for t in range(ts.start, ts.stop):
+                z_rows_of(z_rows[:, t, :], sig[:, t, :], t, slice(b * BLOCK, (b + 1) * BLOCK))
+
+        def second_layer(name, cols, z_rows, acc, on_scalar):
+            n = cols.stop - cols.start
+            z_grouped = keep.tile([P, n, PACK], BF16, name=name + "_grouped", align_bytes=64)
+            z_words = keep.tile([P, n], U32, name=name + "_words", align_bytes=64)
+            z_scales = keep.tile([P, n], U8, name=name + "_scales", align_bytes=64)
+            interleave(on_scalar, z_grouped[:], z_rows[:])
+            nc.vector.quantize_mx(z_words[:].bitcast(FP8X4), z_scales[:], z_grouped[:].rearrange("p j t -> p (j t)"))
+            for t in range(PACK):
+                product(acc[t], w3, t, x2_words[:, cols], x2_scales[:, cols], True, False)
+                product(acc[t], w2, t, z_words[:], z_scales[:], False, True)
+
+        every, low, high = slice(0, PACK), slice(0, 2), slice(2, PACK)
+        mb_left = [look_up_left(t) for t in range(PACK)]
+        mb2 = keep.tile([P, PACK, S], F32, name="mb2")
+        mb3 = keep.tile([P, PACK, S], F32, name="mb3")
+        sig2 = keep.tile([P, PACK, BLOCK], F32, name="sig2")
+        sig3 = keep.tile([P, PACK, BLOCK], F32, name="sig3")
+        z2 = keep.tile([P, PACK, BLOCK], BF16, name="z2")
+        z3 = keep.tile([P, PACK, BLOCK], BF16, name="z3")
+        look_up(2, range(G2_EARLY), mb2)
+        for t, u in LEFT_SCALAR:
+            gather(True, mb_left[t][:, u * S : (u + 1) * S], y[t], entries(n1_t, u * S, S))
+        look_up(2, range(G2_EARLY, PACK), mb2)
+        sums0 = sum_left(0, (0, 1))
+        sums1 = sum_left(2, (2,))
+        back0 = gate_left(1, (0, 1), sums0)
+        sums2 = sum_left(0, (3,))
+        look_up(3, range(G3_A), mb3)
+        back1 = gate_left(3, (2,), sums1)
+        look_up(3, range(G3_A, G3_B), mb3)
+        ms2 = add_members(mb2, every)
+        rows_left((0, 1), back0)
+        rows_left((2,), back1)
+        back2 = gate_left(2, (3,), sums2)
+        gate(ms2, sig2, every)
+        look_up(3, range(G3_B, PACK), mb3)
+        ms3 = add_members(mb3, low)
+        rows_left((3,), back2)
+        gate(ms3, sig3, low)
+        second_layer("left", slice(0, HALF), z_left, [h_left[t][:] for t in range(PACK)], IL_SCALAR[0])
+        rows_right(2, sig2, every, z2)
+        ms3 = add_members(mb3, high)
+        gate(ms3, sig3, high)
+        h_right = [psum.tile([P, S], F32, name="bank_a%d" % t) for t in range(PACK)]
+        second_layer("b2", slice(HALF, HALF + BLOCK), z2, [h_right[t][:, :BLOCK] for t in range(PACK)], IL_SCALAR[1])
+        for t in range(PACK):
+            nc.scalar.activation(h[t][:, :HALF], h_left[t][:], ACT.Copy)
+        rows_right(3, sig3, every, z3)
+        second_layer("b3", slice(HALF + BLOCK, S), z3, [h_right[t][:, BLOCK:HALF] for t in range(PACK)], False)
+
+        for t in (2, 0, 3, 1):
+            if t >= 2:
+                nc.vector.tensor_copy(h[t][:, HALF:S], h_right[t][:, :HALF])
+            else:
+                nc.scalar.activation(h[t][:, HALF:S], h_right[t][:, :HALF], ACT.Copy)
+
+        def fetch(name, win, offsets, on_scalar):
+            got = ring.tile([P, S], F32, name=name, bufs=4)
+            if all(on_scalar):
+                gather(True, got[:], win, offsets[:])
+            else:
+                for u in range(2):
+                    gather(on_scalar[u], got[:, u * HALF : (u + 1) * HALF], win, entries(offsets, u * HALF, HALF))
+            return got
+
+        def step_st(t, got):
+            engine = nc.gpsimd if t in SUB_POOL else nc.vector
+            engine.tensor_tensor(neg_st[t][:, :S], got[:], h[t][:, :S], ALU.subtract)
+
+        def step_su(t, got):
+            nc.vector.tensor_tensor(neg_su[t][:], got[:], neg_st[t][:, :S], ALU.min)
+
+        both, neither = (True, True), (False, False)
+        a2 = fetch("got2", h[2], n2_t, neither)
+        a0 = fetch("got2", h[0], n2_t, both)
+        a1 = fetch("got2", h[1], n2_t, both)
+        step_st(2, a2)
+        a3 = fetch("got2", h[3], n2_t, neither)
+        step_st(0, a0)
+        step_st(1, a1)
+        step_st(3, a3)
+        b2 = fetch("got3", neg_st[2], n3_t, both)
+        b0 = fetch("got3", neg_st[0], n3_t, both)
+        b1 = fetch("got3", neg_st[1], n3_t, both)
+        step_su(2, b2)
+        b3 = fetch("got3", neg_st[3], n3_t, B3)
+        step_su(0, b0)
+        step_su(1, b1)
+        step_su(3, b3)
+
+        out_rows = out_0.rearrange("(p t) j -> p t j", t=PACK)
+        out_words = out_1[0].rearrange("p n t -> p (n t)").bitcast(I32)
+        scales = keep.tile([P, S], U8, name="scales", align_bytes=64)
+        result = [keep.tile([P, PACK, HALF], F32, name="result%d" % u) for u in range(2)]
+
+        def step_out(t, u):
+            got = ring.tile([P, HALF], F32, name="got4", bufs=8)
+            gather((t, u) not in C_VECTOR, got[:], neg_su[t], entries(n4_t, u * HALF, HALF))
+            nc.vector.scalar_tensor_tensor(
+                result[u][:, t, :], got[:], -0.5, neg_su[t][:, u * HALF : (u + 1) * HALF], ALU.mult, ALU.subtract
+            )
+
+        def planes(u):
+            cols = slice(u * HALF, (u + 1) * HALF)
+            grouped = keep.tile([P, HALF, PACK], BF16, name="grouped%d" % u, align_bytes=64)
+            words = keep.tile([P, HALF], U32, name="words%d" % u, align_bytes=64)
+            nc.sync.dma_start(out_rows[:, :, cols], result[u][:])
+            interleave(IL_OUT[u], grouped[:], result[u][:])
+            nc.vector.quantize_mx(words[:].bitcast(FP8X4), scales[:, cols], grouped[:].rearrange("p j t -> p (j t)"))
+            nc.sync.dma_start(out_words[:, cols], words[:].bitcast(I32))
+
+        for t, u in ((2, 0), (0, 0), (1, 0), (3, 0)):
+            step_out(t, u)
+        planes(0)
+        for t in (2, 0, 1, 3):
+            step_out(t, 1)
+        planes(1)
+        for q in range(4):
+            queue = nc.scalar if q < 3 else nc.sync
+            queue.dma_start(out_2[0, 4 * q : 4 * q + 4, :].bitcast(I32), scales[32 * q : 32 * q + 4, :].bitcast(I32))

@@ -15,26 +15,30 @@ ALU = mybir.AluOpType
 ACT = mybir.ActivationFunctionType
 
 P = 128
-PACK = 4
-T = 2048
+SLOTS = 4
+QUADRANTS = 4
+TOKENS = 2048
 S = 512
-MEMBERS = 4
-BLOCK = 128
-BLOCKS = S // BLOCK
 HALF = S // 2
-SPARE = 8
-PER_COL = 16
+QUARTER = S // 4
+MEMBERS = 4
+ENTRIES_PER_COLUMN = 16
+LINE = 4
+ALIGN = 64
 
-IL_SCALAR = (True, True)
-G3_A = 2
-G3_B = 3
-G2_EARLY = 4
-LEFT_SCALAR = ()
-C_VECTOR = ((3, 0),)
-IL_OUT = (True, False)
-SUB_POOL = ()
-WARM = False
-B3 = (False, False)
+LEFT, MID, LAST = slice(0, HALF), slice(HALF, S - QUARTER), slice(S - QUARTER, S)
+HALVES = (slice(0, HALF), slice(HALF, S))
+
+H_ORDER = (2, 0, 3, 1)
+
+AT_X_ROWS = 0
+AT_W1_WORDS = AT_X_ROWS
+AT_W1_SCALES = AT_W1_WORDS + 2 * S
+AT_W_RAW = AT_X_ROWS + TOKENS
+AT_X2_SCALES = AT_W_RAW + 4 * S
+AT_GAIN = AT_X2_SCALES + S
+AT_W23_SCALES = AT_GAIN + ALIGN
+AT_W1_ROWS = AT_GAIN - ALIGN
 
 FLOPS = 3 * 2 * 512 * 512 * 512
 
@@ -47,67 +51,50 @@ def tile_picked_mixingsumgthree_none_po_kernel(
     with ExitStack() as ctx:
         lists = ctx.enter_context(tc.tile_pool(name="lists", bufs=1))
         keep = ctx.enter_context(tc.tile_pool(name="keep", bufs=1))
-        ring = ctx.enter_context(tc.tile_pool(name="ring", bufs=2))
+        stage = ctx.enter_context(tc.tile_pool(name="stage", bufs=1))
         psum = ctx.enter_context(tc.psum_pool(name="psum", bufs=1))
+
+        def staged(name, shape, dtype, offset):
+            return stage.tile(shape, dtype, name=name, offset=offset, align_bytes=ALIGN)
+
+        def aligned(name, shape, dtype):
+            return keep.tile(shape, dtype, name=name, align_bytes=ALIGN)
+
+        def bank(number):
+            return psum.tile([P, S], F32, name="bank%d" % number)
 
         def load_list(name, src):
             tile = lists.tile([P, src.shape[1]], U16, name=name)
             nc.sync.dma_start(tile[:], src)
             return tile
 
-        def load_scale_rows(queues, tile, src):
-            for q in range(4):
-                queues[q].dma_start(tile[32 * q : 32 * q + 4].bitcast(I32), src[0, 4 * q : 4 * q + 4, :].bitcast(I32))
+        def entries(list_tile, first, count):
+            return list_tile[:, first // ENTRIES_PER_COLUMN : (first + count) // ENTRIES_PER_COLUMN]
 
-        def entries(tile, first, count):
-            return tile[:, first // PER_COL : (first + count) // PER_COL]
+        def scale_rows(q):
+            return slice(32 * q, 32 * q + 4)
+
+        def load_scale_rows(queues, dst, src):
+            for q in range(QUADRANTS):
+                queue = queues[q % len(queues)]
+                queue.dma_start(dst[scale_rows(q)].bitcast(I32), src[0, 4 * q : 4 * q + 4, :].bitcast(I32))
+
+        def load_words(queue, dst, src):
+            queue.dma_start(dst.bitcast(I32), src[0].bitcast(I32))
 
         def window(name):
-            tile = keep.tile([P, S + SPARE], F32, name=name)
-            nc.gpsimd.memset(tile[:, S:], 0.0)
+            tile = keep.tile([P, S + 1], F32, name=name)
+            nc.vector.memset(tile[:, S:], 0.0)
             return tile
 
-        def gather(on_scalar, out, win, offsets):
-            if on_scalar:
-                nc.scalar.activation(out, win[:].indirect(offsets), ACT.Copy)
-            else:
-                nc.vector.tensor_copy(out, win[:].indirect(offsets))
+        def scalar_gather(out, win, offsets):
+            nc.scalar.activation(out, win[:].indirect(offsets), ACT.Copy)
 
-        def interleave(on_scalar, dst, src):
-            copy = nc.scalar.copy if on_scalar else nc.vector.tensor_copy
-            copy(dst.rearrange("p (c i) t -> p c t i", i=4), src.rearrange("p t (c i) -> p c t i", i=4))
+        def vector_gather(out, win, offsets):
+            nc.vector.tensor_copy(out, win[:].indirect(offsets))
 
-        xw = keep.tile([P, T], I32, name="xw")
-        xs = keep.tile([P, T], U8, name="xs")
-        raw_w1 = keep.tile([P, 2 * S], U8, name="raw_w1")
-        raw_w23 = keep.tile([P, 2, 2 * S], U8, name="raw_w23")
-        raw_s23 = keep.tile([P, 2, S], U8, name="raw_s23")
-        raw_s1 = raw_w23[:].rearrange("p i n -> p (i n)")[:, 2 * S - S // 2 : 2 * S + S // 2]
-        nc.vector.memset(xs[:].bitcast(I32), 0)
-        nc.vector.memset(raw_s1.bitcast(I32), 0)
-        nc.vector.memset(raw_s23[:].rearrange("p i n -> p (i n)").bitcast(I32), 0)
-
-        def load_words(queue, tile, words):
-            queue.dma_start(tile.bitcast(I32), words[0].bitcast(I32))
-
-        def deal_words(name, raw):
-            words = keep.tile([P, PACK, P, 2], U8, name=name + "_words", align_bytes=64)
-            nc.gpsimd.tensor_copy(words[:], raw.rearrange("p (m t b) -> p t m b", t=PACK, b=2))
-            return words
-
-        def deal_scales(name, raw):
-            scales = keep.tile([P, PACK, P], U8, name=name + "_scales", align_bytes=64)
-            nc.gpsimd.tensor_copy(scales[:], raw.rearrange("p (m t) -> p t m", t=PACK))
-            return scales
-
-        def pick(name, offsets, pieces):
-            scales = keep.tile([P, S], U8, name=name + "_scales", align_bytes=64)
-            words = keep.tile([P, S], U32, name=name + "_words", align_bytes=64)
-            nc.vector.tensor_copy(scales[:], xs[:].indirect(offsets[:]))
-            for u in range(pieces):
-                n = S // pieces
-                nc.vector.tensor_copy(words[:, u * n : (u + 1) * n], xw[:].bitcast(U32).indirect(entries(offsets, u * n, n)))
-            return words, scales
+        def words_by_slot(raw):
+            return raw.rearrange("p (m t b) -> p t m b", t=SLOTS, b=2)
 
         def product(out, weight, t, words, scales, start, stop):
             nc.tensor.matmul_mx(
@@ -120,221 +107,266 @@ def tile_picked_mixingsumgthree_none_po_kernel(
                 stop=stop,
             )
 
-        offs_t = load_list("offs_t", offs)
-        load_words(nc.scalar, raw_w1[:], w1_words)
-        two_t = load_list("two_t", two)
-        load_scale_rows([nc.scalar, nc.scalar, nc.sync, nc.sync], xs[:], x_scales)
-        nc.scalar.dma_start(xw[:], x_words[0].rearrange("p n t -> p (n t)").bitcast(I32))
-        load_scale_rows([nc.sync] * 4, raw_s1, w1_scales)
-        n1_t = load_list("n1_t", n1)
-        load_scale_rows([nc.sync] * 4, raw_s23[:, 0, :], w3_scales)
-        load_scale_rows([nc.sync] * 4, raw_s23[:, 1, :], w2_scales)
-        gain = keep.tile([P, PACK], F32, name="gain")
-        nc.sync.dma_start(gain[:], gn.rearrange("(p t) o -> p (t o)", t=PACK))
-        n2_t = load_list("n2_t", n2)
-        n3_t = load_list("n3_t", n3)
-        n4_t = load_list("n4_t", n4)
+        def group(name, copy, by_slot):
+            grouped = aligned(name + "_grouped", [P, by_slot.shape[2], SLOTS], BF16)
+            copy(
+                grouped[:].rearrange("p (c i) t -> p c t i", i=LINE),
+                by_slot.rearrange("p t (c i) -> p c t i", i=LINE),
+            )
+            return grouped
 
-        y = [window("y%d" % t) for t in range(PACK)]
-        h = [window("h%d" % t) for t in range(PACK)]
-        neg_st = [window("neg_st%d" % t) for t in range(PACK)]
-        neg_su = [keep.tile([P, S], F32, name="neg_su%d" % t) for t in range(PACK)]
+        def quantise(words, scales, grouped):
+            nc.vector.quantize_mx(words.bitcast(FP8X4), scales, grouped[:].rearrange("p j t -> p (j t)"))
 
-        if WARM:
-            warm = keep.tile([P, SPARE], F32, name="warm")
-            nc.scalar.activation(warm[:], y[0][:, S:], ACT.Sigmoid)
-        ident = keep.tile([P, P], F32, name="ident")
-        make_identity(nc, ident[:])
+        x_word_table = keep.tile([P, TOKENS], I32, name="x_word_table")
+        x_scale_table = keep.tile([P, TOKENS], U8, name="x_scale_table")
+        x_rows = staged("x_rows", [P, TOKENS], U8, AT_X_ROWS)
+        w1_raw = staged("w1_raw", [P, 2 * S], U8, AT_W_RAW)
+        w1_rows = staged("w1_rows", [P, S], U8, AT_W1_ROWS)
+        w23_rows = keep.tile([P, 2, S], U8, name="w23_rows")
+        nc.vector.memset(w1_rows[:].bitcast(I32), 0)
+        nc.gpsimd.memset(x_scale_table[:].bitcast(I32), 0)
+        nc.vector.memset(w23_rows[:].rearrange("p i n -> p (i n)").bitcast(I32), 0)
 
-        w1 = (deal_words("w1", raw_w1[:]), deal_scales("w1", raw_s1))
-        load_words(nc.sync, raw_w23[:, 0, :], w3_words)
-        load_words(nc.sync, raw_w23[:, 1, :], w2_words)
-        x1_words, x1_scales = pick("x1", offs_t, 2)
-        y_banks = [psum.tile([P, S], F32, name="bank_a%d" % t) for t in range(PACK)]
-        for t in range(PACK):
-            for u in range(2):
-                cols = slice(u * HALF, (u + 1) * HALF)
-                product(y_banks[t][:, cols], w1, t, x1_words[:, cols], x1_scales[:, cols], True, True)
-            nc.scalar.activation(y[t][:, :S], y_banks[t][:], ACT.Copy)
+        load_scale_rows([nc.sync, nc.scalar], x_rows[:], x_scales)
+        offs_list = load_list("offs_list", offs)
+        load_words(nc.scalar, w1_raw[:], w1_words)
+        nc.sync.dma_start(x_word_table[:], x_words[0].rearrange("p n t -> p (n t)").bitcast(I32))
+        load_scale_rows([nc.scalar, nc.sync], w1_rows[:], w1_scales)
+        two_list = load_list("two_list", two)
+        n1_list = load_list("n1_list", n1)
+        load_scale_rows([nc.sync], w23_rows[:, 0, :], w3_scales)
+        load_scale_rows([nc.sync], w23_rows[:, 1, :], w2_scales)
+        n2_list = load_list("n2_list", n2)
+        n3_list = load_list("n3_list", n3)
+        n4_list = load_list("n4_list", n4)
 
-        x2_words, x2_scales = pick("x2", two_t, 1)
-        w3 = (deal_words("w3", raw_w23[:, 0, :]), deal_scales("w3", raw_s23[:, 0, :]))
-        w2 = (deal_words("w2", raw_w23[:, 1, :]), deal_scales("w2", raw_s23[:, 1, :]))
+        for q in range(QUADRANTS):
+            nc.vector.tensor_copy(x_scale_table[scale_rows(q), :].bitcast(I32), x_rows[scale_rows(q), :].bitcast(I32))
+        y = [window("y%d" % t) for t in range(SLOTS)]
+        h = [window("h%d" % t) for t in range(SLOTS)]
+        neg_st = [window("neg_st%d" % t) for t in range(SLOTS)]
 
-        h_left = [psum.tile([P, HALF], F32, name="bank_b%d" % t) for t in range(PACK)]
-        z_left = keep.tile([P, PACK, HALF], BF16, name="z_left")
+        warm = keep.tile([P, 1], F32, name="warm")
+        nc.scalar.activation(warm[:], y[0][:, S:], ACT.Sigmoid)
+        identity = keep.tile([P, P], F32, name="identity")
+        make_identity(nc, identity[:])
 
-        def look_up_left(t):
-            mb = ring.tile([P, HALF * MEMBERS], F32, name="mb_left", bufs=PACK)
-            for u in range(2):
-                if (t, u) not in LEFT_SCALAR:
-                    gather(False, mb[:, u * S : (u + 1) * S], y[t], entries(n1_t, u * S, S))
-            return mb
+        w1 = (staged("w1_dealt", [P, SLOTS, P, 2], U8, AT_W1_WORDS), staged("w1_dealt_scales", [P, SLOTS, P], U8, AT_W1_SCALES))
+        nc.gpsimd.tensor_copy(w1[0][:, :2, :, :], words_by_slot(w1_raw[:])[:, :2, :, :])
+        nc.gpsimd.tensor_copy(w1[1][:], w1_rows[:].rearrange("p (m t) -> p t m", t=SLOTS))
+        nc.gpsimd.tensor_copy(w1[0][:, 2:, :, :], words_by_slot(w1_raw[:])[:, 2:, :, :])
 
-        def sum_left(bank, ts):
-            sums = psum.tile([P, S], F32, name="bank_a%d" % bank)
-            for c in range(2 * len(ts)):
-                members = mb_left[ts[c // 2]][:, (c % 2) * S : (c % 2 + 1) * S]
+        w23_raw = staged("w23_raw", [P, 2, 2 * S], U8, AT_W_RAW)
+        gain = staged("gain", [P, SLOTS], F32, AT_GAIN)
+        nc.sync.dma_start(gain[:], gn.rearrange("(p t) o -> p (t o)", t=SLOTS))
+        load_words(nc.sync, w23_raw[:, 0, :], w3_words)
+        load_words(nc.sync, w23_raw[:, 1, :], w2_words)
+
+        def pick_words(out, list_tile, cols):
+            nc.vector.tensor_copy(out, x_word_table[:].bitcast(U32).indirect(entries(list_tile, cols.start, HALF)))
+
+        x1_scales = aligned("x1_scales", [P, S], U8)
+        x1_words = aligned("x1_words", [P, S], U32)
+        vector_gather(x1_scales[:], x_scale_table, offs_list[:])
+        for cols in HALVES:
+            pick_words(x1_words[:, cols], offs_list, cols)
+        for t in range(SLOTS):
+            y_bank = bank(t)
+            for cols in HALVES:
+                product(y_bank[:, cols], w1, t, x1_words[:, cols], x1_scales[:, cols], True, True)
+            nc.scalar.activation(y[t][:, :S], y_bank[:], ACT.Copy)
+
+        x2_scales = staged("x2_scales", [P, S], U8, AT_X2_SCALES)
+        x2_left = aligned("x2_left", [P, HALF], U32)
+        vector_gather(x2_scales[:], x_scale_table, two_list[:])
+        pick_words(x2_left[:], two_list, HALVES[0])
+
+        w23_scales = staged("w23_scales", [P, 2, SLOTS, P], U8, AT_W23_SCALES)
+        w3 = (aligned("w3_dealt", [P, SLOTS, P, 2], U8), w23_scales[:, 0, :, :])
+        w2 = (aligned("w2_dealt", [P, SLOTS, P, 2], U8), w23_scales[:, 1, :, :])
+        nc.gpsimd.tensor_copy(w23_scales[:], w23_rows[:].rearrange("p i (m t) -> p i t m", t=SLOTS))
+        nc.gpsimd.tensor_copy(w3[0][:], words_by_slot(w23_raw[:, 0, :]))
+        nc.gpsimd.tensor_copy(w2[0][:], words_by_slot(w23_raw[:, 1, :]))
+
+        shared = [(quarter, (t,)) for t in range(SLOTS) for quarter in range(2)]
+        shared = shared + [(2, (0, 1, 2, 3)), (3, (0, 1)), (3, (2,)), (3, (3,))]
+        member_tiles = {
+            (quarter, slots): keep.tile([P, len(slots), S], F32, name="members%d_%d" % (quarter, slots[0]))
+            for quarter, slots in shared
+        }
+        members = {(quarter, t): member_tiles[quarter, slots][:, i, :] for quarter, slots in shared for i, t in enumerate(slots)}
+        gates_mid = keep.tile([P, SLOTS, QUARTER], F32, name="gates_mid")
+        gates_last = keep.tile([P, SLOTS, QUARTER], F32, name="gates_last")
+        z_left = keep.tile([P, SLOTS, HALF], BF16, name="z_left")
+        z_mid = keep.tile([P, SLOTS, QUARTER], BF16, name="z_mid")
+        z_last = keep.tile([P, SLOTS, QUARTER], BF16, name="z_last")
+
+        def look_up(gather, quarter, t):
+            gather(members[quarter, t], y[t], entries(n1_list, quarter * S, S))
+
+        def sum_on_tensor(number, slots):
+            sums = bank(number)
+            pieces = [members[quarter, t] for t in slots for quarter in range(2)]
+            for c, piece in enumerate(pieces):
                 for d in range(MEMBERS):
                     nc.tensor.matmul(
-                        sums[:, c * P : (c + 1) * P], lhsT=members[:, d::MEMBERS], rhs=ident[:],
+                        sums[:, c * P : (c + 1) * P], lhsT=piece[:, d::MEMBERS], rhs=identity[:],
                         is_transpose=True, start=d == 0, stop=d == MEMBERS - 1,
                     )
+            return sums[:, : len(pieces) * P]
+
+        def gate_and_turn_back(number, sums, name):
+            width = sums.shape[1]
+            gates = bank(number)
+            turned = aligned(name, [P, S], F32)
+            nc.scalar.activation(turned[:, :width], sums, ACT.Sigmoid)
+            for c in range(width // P):
+                nc.tensor.transpose(gates[:, c * P : (c + 1) * P], turned[:, c * P : (c + 1) * P], identity[:])
+            return gates
+
+        def sum_on_vector(quarter, slots):
+            width = len(slots) * QUARTER
+            pairs = keep.tile([P, width, 2], F32, name="pairs%d_%d" % (quarter, slots[0]))
+            sums = keep.tile([P, width], F32, name="sums%d_%d" % (quarter, slots[0]))
+            fours = member_tiles[quarter, slots][:].rearrange("p t (j d) -> p (t j) d", d=MEMBERS)
+            nc.vector.tensor_tensor(pairs[:], fours[:, :, 0:2], fours[:, :, 2:4], ALU.add)
+            nc.vector.tensor_tensor(sums[:], pairs[:, :, 0], pairs[:, :, 1], ALU.add)
             return sums
 
-        def gate_left(bank, ts, sums):
-            n = HALF * len(ts)
-            back = psum.tile([P, S], F32, name="bank_a%d" % bank)
-            turned = ring.tile([P, S], F32, name="turned", bufs=3)
-            nc.scalar.activation(turned[:, :n], sums[:, :n], ACT.Sigmoid)
-            for c in range(2 * len(ts)):
-                nc.tensor.transpose(back[:, c * P : (c + 1) * P], turned[:, c * P : (c + 1) * P], ident[:])
-            return back
+        def gate(gates, slots, sums):
+            nc.scalar.activation(gates[:, slots[0] : slots[-1] + 1, :].rearrange("p t j -> p (t j)"), sums[:], ACT.Sigmoid)
 
-        def z_rows_of(dst, sig, t, cols):
-            nc.vector.scalar_tensor_tensor(dst, sig, gain[:, t : t + 1], y[t][:, cols], ALU.mult, ALU.mult)
+        def z_slot(z, t, gates, cols):
+            nc.vector.scalar_tensor_tensor(z[:, t, :], gates, gain[:, t : t + 1], y[t][:, cols], ALU.mult, ALU.mult)
 
-        def rows_left(ts, back):
-            for i, t in enumerate(ts):
-                z_rows_of(z_left[:, t, :], back[:, i * HALF : (i + 1) * HALF], t, slice(0, HALF))
+        def z_operand(name, grouped):
+            width = grouped.shape[1]
+            words, scales = aligned(name + "_words", [P, width], U32), aligned(name + "_scales", [P, width], U8)
+            quantise(words[:], scales[:], grouped)
+            return words[:], scales[:]
 
-        def look_up(b, ts, mb):
-            for t in ts:
-                gather(True, mb[:, t, :], y[t], entries(n1_t, b * BLOCK * MEMBERS, BLOCK * MEMBERS))
+        def passes(banks, cols, weight, words, scales, start, stop):
+            for t in H_ORDER:
+                product(banks[t][:, cols], weight, t, words, scales, start, stop)
 
-        def add_members(mb, ts):
-            n = (ts.stop - ts.start) * BLOCK
-            pairs = ring.tile([P, n, 2], F32, name="pairs", bufs=3)
-            ms = ring.tile([P, n], F32, name="ms", bufs=3)
-            members = mb[:, ts, :].rearrange("p t (j d) -> p (t j) d", d=MEMBERS)
-            nc.vector.tensor_tensor(pairs[:], members[:, :, 0:2], members[:, :, 2:4], ALU.add)
-            nc.vector.tensor_tensor(ms[:], pairs[:, :, 0], pairs[:, :, 1], ALU.add)
-            return ms
+        left_pieces = [(quarter, t) for t in range(SLOTS) for quarter in range(2)]
+        for quarter, t in left_pieces[:-1]:
+            look_up(vector_gather, quarter, t)
+        for t in range(SLOTS):
+            look_up(scalar_gather, 2, t)
+        sums01 = sum_on_tensor(0, (0, 1))
+        sums2 = sum_on_tensor(2, (2,))
+        gates01 = gate_and_turn_back(1, sums01, "turned01")
+        look_up(scalar_gather, *left_pieces[-1])
+        sums3 = sum_on_tensor(0, (3,))
 
-        def gate(ms, sig, ts):
-            nc.scalar.activation(sig[:, ts, :].rearrange("p t j -> p (t j)"), ms[:], ACT.Sigmoid)
+        for t in (0, 1):
+            look_up(scalar_gather, 3, t)
+        sums_mid = sum_on_vector(2, (0, 1, 2, 3))
+        for t in (0, 1):
+            z_slot(z_left, t, gates01[:, t * HALF : (t + 1) * HALF], LEFT)
+        x2_right = aligned("turned01", [P, HALF], U32)
+        pick_words(x2_right[:], two_list, HALVES[1])
+        gate(gates_mid, (0, 1, 2, 3), sums_mid)
+        gates2 = gate_and_turn_back(3, sums2, "turned2")
+        sums_last01 = sum_on_vector(3, (0, 1))
+        gates3 = gate_and_turn_back(2, sums3, "turned3")
+        for t in (2, 3):
+            look_up(scalar_gather, 3, t)
+        gate(gates_last, (0, 1), sums_last01)
+        for t in range(SLOTS):
+            z_slot(z_mid, t, gates_mid[:, t, :], MID)
+        mid_grouped = group("z_mid", nc.vector.tensor_copy, z_mid[:])
+        z_slot(z_left, 2, gates2[:, :HALF], LEFT)
+        mid_operand = z_operand("z_mid", mid_grouped)
+        z_slot(z_left, 3, gates3[:, :HALF], LEFT)
 
-        def rows_right(b, sig, ts, z_rows):
-            for t in range(ts.start, ts.stop):
-                z_rows_of(z_rows[:, t, :], sig[:, t, :], t, slice(b * BLOCK, (b + 1) * BLOCK))
+        h_early = {t: bank(number) for t, number in zip(H_ORDER, (1, 0, 3, 2))}
+        h_late = [bank(SLOTS + t) for t in range(SLOTS)]
+        late_cols = slice(0, QUARTER)
+        passes(h_early, LEFT, w3, x2_left[:], x2_scales[:, LEFT], True, False)
+        passes(h_early, MID, w3, x2_right[:, :QUARTER], x2_scales[:, MID], False, False)
+        passes(h_late, late_cols, w3, x2_right[:, QUARTER:], x2_scales[:, LAST], True, False)
+        passes(h_early, MID, w2, *mid_operand, False, False)
+        left_grouped = group("z_left", nc.vector.tensor_copy, z_left[:])
+        for t in (2, 3):
+            gate(gates_last, (t,), sum_on_vector(3, (t,)))
+        passes(h_early, LEFT, w2, *z_operand("z_left", left_grouped), False, True)
+        for t in range(SLOTS):
+            z_slot(z_last, t, gates_last[:, t, :], LAST)
+        passes(h_late, late_cols, w2, *z_operand("z_last", group("z_last", nc.vector.tensor_copy, z_last[:])), False, True)
 
-        def second_layer(name, cols, z_rows, acc, on_scalar):
-            n = cols.stop - cols.start
-            z_grouped = keep.tile([P, n, PACK], BF16, name=name + "_grouped", align_bytes=64)
-            z_words = keep.tile([P, n], U32, name=name + "_words", align_bytes=64)
-            z_scales = keep.tile([P, n], U8, name=name + "_scales", align_bytes=64)
-            interleave(on_scalar, z_grouped[:], z_rows[:])
-            nc.vector.quantize_mx(z_words[:].bitcast(FP8X4), z_scales[:], z_grouped[:].rearrange("p j t -> p (j t)"))
-            for t in range(PACK):
-                product(acc[t], w3, t, x2_words[:, cols], x2_scales[:, cols], True, False)
-                product(acc[t], w2, t, z_words[:], z_scales[:], False, True)
-
-        every, low, high = slice(0, PACK), slice(0, 2), slice(2, PACK)
-        mb_left = [look_up_left(t) for t in range(PACK)]
-        mb2 = keep.tile([P, PACK, S], F32, name="mb2")
-        mb3 = keep.tile([P, PACK, S], F32, name="mb3")
-        sig2 = keep.tile([P, PACK, BLOCK], F32, name="sig2")
-        sig3 = keep.tile([P, PACK, BLOCK], F32, name="sig3")
-        z2 = keep.tile([P, PACK, BLOCK], BF16, name="z2")
-        z3 = keep.tile([P, PACK, BLOCK], BF16, name="z3")
-        look_up(2, range(G2_EARLY), mb2)
-        for t, u in LEFT_SCALAR:
-            gather(True, mb_left[t][:, u * S : (u + 1) * S], y[t], entries(n1_t, u * S, S))
-        look_up(2, range(G2_EARLY, PACK), mb2)
-        sums0 = sum_left(0, (0, 1))
-        sums1 = sum_left(2, (2,))
-        back0 = gate_left(1, (0, 1), sums0)
-        sums2 = sum_left(0, (3,))
-        look_up(3, range(G3_A), mb3)
-        back1 = gate_left(3, (2,), sums1)
-        look_up(3, range(G3_A, G3_B), mb3)
-        ms2 = add_members(mb2, every)
-        rows_left((0, 1), back0)
-        rows_left((2,), back1)
-        back2 = gate_left(2, (3,), sums2)
-        gate(ms2, sig2, every)
-        look_up(3, range(G3_B, PACK), mb3)
-        ms3 = add_members(mb3, low)
-        rows_left((3,), back2)
-        gate(ms3, sig3, low)
-        second_layer("left", slice(0, HALF), z_left, [h_left[t][:] for t in range(PACK)], IL_SCALAR[0])
-        rows_right(2, sig2, every, z2)
-        ms3 = add_members(mb3, high)
-        gate(ms3, sig3, high)
-        h_right = [psum.tile([P, S], F32, name="bank_a%d" % t) for t in range(PACK)]
-        second_layer("b2", slice(HALF, HALF + BLOCK), z2, [h_right[t][:, :BLOCK] for t in range(PACK)], IL_SCALAR[1])
-        for t in range(PACK):
-            nc.scalar.activation(h[t][:, :HALF], h_left[t][:], ACT.Copy)
-        rows_right(3, sig3, every, z3)
-        second_layer("b3", slice(HALF + BLOCK, S), z3, [h_right[t][:, BLOCK:HALF] for t in range(PACK)], False)
-
-        for t in (2, 0, 3, 1):
-            if t >= 2:
-                nc.vector.tensor_copy(h[t][:, HALF:S], h_right[t][:, :HALF])
+        for t in H_ORDER:
+            nc.scalar.activation(h[t][:, : LAST.start], h_early[t][:, : LAST.start], ACT.Copy)
+        for t in H_ORDER:
+            if t < 2:
+                nc.scalar.activation(h[t][:, LAST], h_late[t][:, late_cols], ACT.Copy)
             else:
-                nc.scalar.activation(h[t][:, HALF:S], h_right[t][:, :HALF], ACT.Copy)
+                nc.vector.tensor_copy(h[t][:, LAST], h_late[t][:, late_cols])
 
-        def fetch(name, win, offsets, on_scalar):
-            got = ring.tile([P, S], F32, name=name, bufs=4)
-            if all(on_scalar):
-                gather(True, got[:], win, offsets[:])
-            else:
-                for u in range(2):
-                    gather(on_scalar[u], got[:, u * HALF : (u + 1) * HALF], win, entries(offsets, u * HALF, HALF))
-            return got
+        neg_su = [keep.tile([P, S], F32, name="neg_su%d" % t) for t in range(SLOTS)]
 
-        def step_st(t, got):
-            engine = nc.gpsimd if t in SUB_POOL else nc.vector
-            engine.tensor_tensor(neg_st[t][:, :S], got[:], h[t][:, :S], ALU.subtract)
+        def fetch_on_scalar(name, win, list_tile):
+            fetched = keep.tile([P, S], F32, name=name)
+            scalar_gather(fetched[:], win, list_tile[:])
+            return fetched
 
-        def step_su(t, got):
-            nc.vector.tensor_tensor(neg_su[t][:], got[:], neg_st[t][:, :S], ALU.min)
+        def fetch_on_vector(name, win, list_tile):
+            fetched = keep.tile([P, S], F32, name=name)
+            for cols in HALVES:
+                vector_gather(fetched[:, cols], win, entries(list_tile, cols.start, HALF))
+            return fetched
 
-        both, neither = (True, True), (False, False)
-        a2 = fetch("got2", h[2], n2_t, neither)
-        a0 = fetch("got2", h[0], n2_t, both)
-        a1 = fetch("got2", h[1], n2_t, both)
-        step_st(2, a2)
-        a3 = fetch("got2", h[3], n2_t, neither)
-        step_st(0, a0)
-        step_st(1, a1)
-        step_st(3, a3)
-        b2 = fetch("got3", neg_st[2], n3_t, both)
-        b0 = fetch("got3", neg_st[0], n3_t, both)
-        b1 = fetch("got3", neg_st[1], n3_t, both)
-        step_su(2, b2)
-        b3 = fetch("got3", neg_st[3], n3_t, B3)
-        step_su(0, b0)
-        step_su(1, b1)
-        step_su(3, b3)
+        def make_neg_st(t, fetched):
+            nc.vector.tensor_tensor(neg_st[t][:, :S], fetched[:], h[t][:, :S], ALU.subtract)
 
-        out_rows = out_0.rearrange("(p t) j -> p t j", t=PACK)
+        def make_neg_su(t, fetched):
+            nc.vector.tensor_tensor(neg_su[t][:], fetched[:], neg_st[t][:, :S], ALU.min)
+
+        by_n2 = {2: fetch_on_vector("by_n2_2", h[2], n2_list)}
+        for t in (0, 1):
+            by_n2[t] = fetch_on_scalar("by_n2_%d" % t, h[t], n2_list)
+        make_neg_st(2, by_n2[2])
+        by_n2[3] = fetch_on_vector("by_n2_3", h[3], n2_list)
+        for t in (0, 1, 3):
+            make_neg_st(t, by_n2[t])
+        by_n3 = {t: fetch_on_scalar("by_n3_%d" % t, neg_st[t], n3_list) for t in (2, 0, 1)}
+        make_neg_su(2, by_n3[2])
+        by_n3[3] = fetch_on_vector("by_n3_3", neg_st[3], n3_list)
+        for t in (0, 1, 3):
+            make_neg_su(t, by_n3[t])
+
+        result = keep.tile([P, SLOTS, S], F32, name="result")
+        out_rows = out_0.rearrange("(p t) j -> p t j", t=SLOTS)
+
+        def make_result(gather, t, cols):
+            fetched = keep.tile([P, HALF], F32, name="by_n4_%d_%d" % (t, cols.start))
+            gather(fetched[:], neg_su[t], entries(n4_list, cols.start, HALF))
+            nc.vector.scalar_tensor_tensor(result[:, t, cols], fetched[:], -0.5, neg_su[t][:, cols], ALU.mult, ALU.subtract)
+
+        def store_result(t):
+            nc.sync.dma_start(out_rows[:, t, :], result[:, t, :])
+
+        for t in (2, 0):
+            for cols in HALVES:
+                make_result(scalar_gather, t, cols)
+            store_result(t)
+        make_result(vector_gather, 3, HALVES[0])
+        for cols in HALVES:
+            make_result(scalar_gather, 1, cols)
+        store_result(1)
+        make_result(scalar_gather, 3, HALVES[1])
+        store_result(3)
+
         out_words = out_1[0].rearrange("p n t -> p (n t)").bitcast(I32)
-        scales = keep.tile([P, S], U8, name="scales", align_bytes=64)
-        result = [keep.tile([P, PACK, HALF], F32, name="result%d" % u) for u in range(2)]
-
-        def step_out(t, u):
-            got = ring.tile([P, HALF], F32, name="got4", bufs=8)
-            gather((t, u) not in C_VECTOR, got[:], neg_su[t], entries(n4_t, u * HALF, HALF))
-            nc.vector.scalar_tensor_tensor(
-                result[u][:, t, :], got[:], -0.5, neg_su[t][:, u * HALF : (u + 1) * HALF], ALU.mult, ALU.subtract
-            )
-
-        def planes(u):
-            cols = slice(u * HALF, (u + 1) * HALF)
-            grouped = keep.tile([P, HALF, PACK], BF16, name="grouped%d" % u, align_bytes=64)
-            words = keep.tile([P, HALF], U32, name="words%d" % u, align_bytes=64)
-            nc.sync.dma_start(out_rows[:, :, cols], result[u][:])
-            interleave(IL_OUT[u], grouped[:], result[u][:])
-            nc.vector.quantize_mx(words[:].bitcast(FP8X4), scales[:, cols], grouped[:].rearrange("p j t -> p (j t)"))
+        out_scales = aligned("out_scales", [P, S], U8)
+        first_grouped = group("out_first", nc.scalar.copy, result[:, :, HALVES[0]])
+        second_grouped = group("out_second", nc.vector.tensor_copy, result[:, :, HALVES[1]])
+        for name, cols, grouped in (("second", HALVES[1], second_grouped), ("first", HALVES[0], first_grouped)):
+            words = aligned("out_words_" + name, [P, HALF], U32)
+            quantise(words[:], out_scales[:, cols], grouped)
             nc.sync.dma_start(out_words[:, cols], words[:].bitcast(I32))
-
-        for t, u in ((2, 0), (0, 0), (1, 0), (3, 0)):
-            step_out(t, u)
-        planes(0)
-        for t in (2, 0, 1, 3):
-            step_out(t, 1)
-        planes(1)
-        for q in range(4):
-            queue = nc.scalar if q < 3 else nc.sync
-            queue.dma_start(out_2[0, 4 * q : 4 * q + 4, :].bitcast(I32), scales[32 * q : 32 * q + 4, :].bitcast(I32))
+        for q in range(QUADRANTS):
+            queue = nc.sync if q == QUADRANTS - 1 else nc.scalar
+            queue.dma_start(out_2[0, 4 * q : 4 * q + 4, :].bitcast(I32), out_scales[scale_rows(q), :].bitcast(I32))

from contextlib import ExitStack

import concourse.mybir as mybir
from concourse.masks import make_identity

F32 = mybir.dt.float32
BF16 = mybir.dt.bfloat16
I32 = mybir.dt.int32
U32 = mybir.dt.uint32
U16 = mybir.dt.uint16
U8 = mybir.dt.uint8
FP8X4 = mybir.dt.float8_e4m3fn_x4
FP4X4 = mybir.dt.float4_e2m1fn_x4
ALU = mybir.AluOpType
ACT = mybir.ActivationFunctionType

P = 128
SLOTS = 4
QUADRANTS = 4
TOKENS = 2048
S = 512
HALF = S // 2
QUARTER = S // 4
MEMBERS = 4
ENTRIES_PER_COLUMN = 16
LINE = 4
ALIGN = 64

LEFT, MID, LAST = slice(0, HALF), slice(HALF, S - QUARTER), slice(S - QUARTER, S)
HALVES = (slice(0, HALF), slice(HALF, S))

H_ORDER = (2, 0, 3, 1)

AT_X_ROWS = 0
AT_W1_WORDS = AT_X_ROWS
AT_W1_SCALES = AT_W1_WORDS + 2 * S
AT_W_RAW = AT_X_ROWS + TOKENS
AT_X2_SCALES = AT_W_RAW + 4 * S
AT_GAIN = AT_X2_SCALES + S
AT_W23_SCALES = AT_GAIN + ALIGN
AT_W1_ROWS = AT_GAIN - ALIGN

FLOPS = 3 * 2 * 512 * 512 * 512


def tile_picked_mixingsumgthree_none_po_kernel(
    tc, x_words, x_scales, w1_words, w1_scales, gn, w2_words, w2_scales, w3_words, w3_scales,
    offs, n1, two, n2, n3, n4, out_0, out_1, out_2,
):
    nc = tc.nc
    with ExitStack() as ctx:
        lists = ctx.enter_context(tc.tile_pool(name="lists", bufs=1))
        keep = ctx.enter_context(tc.tile_pool(name="keep", bufs=1))
        stage = ctx.enter_context(tc.tile_pool(name="stage", bufs=1))
        psum = ctx.enter_context(tc.psum_pool(name="psum", bufs=1))

        def staged(name, shape, dtype, offset):
            return stage.tile(shape, dtype, name=name, offset=offset, align_bytes=ALIGN)

        def aligned(name, shape, dtype):
            return keep.tile(shape, dtype, name=name, align_bytes=ALIGN)

        def bank(number):
            return psum.tile([P, S], F32, name="bank%d" % number)

        def load_list(name, src):
            tile = lists.tile([P, src.shape[1]], U16, name=name)
            nc.sync.dma_start(tile[:], src)
            return tile

        def entries(list_tile, first, count):
            return list_tile[:, first // ENTRIES_PER_COLUMN : (first + count) // ENTRIES_PER_COLUMN]

        def scale_rows(q):
            return slice(32 * q, 32 * q + 4)

        def load_scale_rows(queues, dst, src):
            for q in range(QUADRANTS):
                queue = queues[q % len(queues)]
                queue.dma_start(dst[scale_rows(q)].bitcast(I32), src[0, 4 * q : 4 * q + 4, :].bitcast(I32))

        def load_words(queue, dst, src):
            queue.dma_start(dst.bitcast(I32), src[0].bitcast(I32))

        def window(name):
            tile = keep.tile([P, S + 1], F32, name=name)
            nc.vector.memset(tile[:, S:], 0.0)
            return tile

        def scalar_gather(out, win, offsets):
            nc.scalar.activation(out, win[:].indirect(offsets), ACT.Copy)

        def vector_gather(out, win, offsets):
            nc.vector.tensor_copy(out, win[:].indirect(offsets))

        def words_by_slot(raw):
            return raw.rearrange("p (m t b) -> p t m b", t=SLOTS, b=2)

        def product(out, weight, t, words, scales, start, stop):
            nc.tensor.matmul_mx(
                out,
                lhsT=weight[0][:, t, :, :].rearrange("p m b -> p (m b)").bitcast(FP4X4),
                lhsT_scale=weight[1][:, t, :],
                rhs=words.bitcast(FP8X4),
                rhs_scale=scales,
                start=start,
                stop=stop,
            )

        def group(name, copy, by_slot):
            grouped = aligned(name + "_grouped", [P, by_slot.shape[2], SLOTS], BF16)
            copy(
                grouped[:].rearrange("p (c i) t -> p c t i", i=LINE),
                by_slot.rearrange("p t (c i) -> p c t i", i=LINE),
            )
            return grouped

        def quantise(words, scales, grouped):
            nc.vector.quantize_mx(words.bitcast(FP8X4), scales, grouped[:].rearrange("p j t -> p (j t)"))

        x_word_table = keep.tile([P, TOKENS], I32, name="x_word_table")
        x_scale_table = keep.tile([P, TOKENS], U8, name="x_scale_table")
        x_rows = staged("x_rows", [P, TOKENS], U8, AT_X_ROWS)
        w1_raw = staged("w1_raw", [P, 2 * S], U8, AT_W_RAW)
        w1_rows = staged("w1_rows", [P, S], U8, AT_W1_ROWS)
        w23_rows = keep.tile([P, 2, S], U8, name="w23_rows")
        nc.vector.memset(w1_rows[:].bitcast(I32), 0)
        nc.gpsimd.memset(x_scale_table[:].bitcast(I32), 0)
        nc.vector.memset(w23_rows[:].rearrange("p i n -> p (i n)").bitcast(I32), 0)

        load_scale_rows([nc.sync, nc.scalar], x_rows[:], x_scales)
        offs_list = load_list("offs_list", offs)
        load_words(nc.scalar, w1_raw[:], w1_words)
        nc.sync.dma_start(x_word_table[:], x_words[0].rearrange("p n t -> p (n t)").bitcast(I32))
        load_scale_rows([nc.scalar, nc.sync], w1_rows[:], w1_scales)
        two_list = load_list("two_list", two)
        n1_list = load_list("n1_list", n1)
        load_scale_rows([nc.sync], w23_rows[:, 0, :], w3_scales)
        load_scale_rows([nc.sync], w23_rows[:, 1, :], w2_scales)
        n2_list = load_list("n2_list", n2)
        n3_list = load_list("n3_list", n3)
        n4_list = load_list("n4_list", n4)

        for q in range(QUADRANTS):
            nc.vector.tensor_copy(x_scale_table[scale_rows(q), :].bitcast(I32), x_rows[scale_rows(q), :].bitcast(I32))
        y = [window("y%d" % t) for t in range(SLOTS)]
        h = [window("h%d" % t) for t in range(SLOTS)]
        neg_st = [window("neg_st%d" % t) for t in range(SLOTS)]

        warm = keep.tile([P, 1], F32, name="warm")
        nc.scalar.activation(warm[:], y[0][:, S:], ACT.Sigmoid)
        identity = keep.tile([P, P], F32, name="identity")
        make_identity(nc, identity[:])

        w1 = (staged("w1_dealt", [P, SLOTS, P, 2], U8, AT_W1_WORDS), staged("w1_dealt_scales", [P, SLOTS, P], U8, AT_W1_SCALES))
        nc.gpsimd.tensor_copy(w1[0][:, :2, :, :], words_by_slot(w1_raw[:])[:, :2, :, :])
        nc.gpsimd.tensor_copy(w1[1][:], w1_rows[:].rearrange("p (m t) -> p t m", t=SLOTS))
        nc.gpsimd.tensor_copy(w1[0][:, 2:, :, :], words_by_slot(w1_raw[:])[:, 2:, :, :])

        w23_raw = staged("w23_raw", [P, 2, 2 * S], U8, AT_W_RAW)
        gain = staged("gain", [P, SLOTS], F32, AT_GAIN)
        nc.sync.dma_start(gain[:], gn.rearrange("(p t) o -> p (t o)", t=SLOTS))
        load_words(nc.sync, w23_raw[:, 0, :], w3_words)
        load_words(nc.sync, w23_raw[:, 1, :], w2_words)

        def pick_words(out, list_tile, cols):
            nc.vector.tensor_copy(out, x_word_table[:].bitcast(U32).indirect(entries(list_tile, cols.start, HALF)))

        x1_scales = aligned("x1_scales", [P, S], U8)
        x1_words = aligned("x1_words", [P, S], U32)
        vector_gather(x1_scales[:], x_scale_table, offs_list[:])
        for cols in HALVES:
            pick_words(x1_words[:, cols], offs_list, cols)
        for t in range(SLOTS):
            y_bank = bank(t)
            for cols in HALVES:
                product(y_bank[:, cols], w1, t, x1_words[:, cols], x1_scales[:, cols], True, True)
            nc.scalar.activation(y[t][:, :S], y_bank[:], ACT.Copy)

        x2_scales = staged("x2_scales", [P, S], U8, AT_X2_SCALES)
        x2_left = aligned("x2_left", [P, HALF], U32)
        vector_gather(x2_scales[:], x_scale_table, two_list[:])
        pick_words(x2_left[:], two_list, HALVES[0])

        w23_scales = staged("w23_scales", [P, 2, SLOTS, P], U8, AT_W23_SCALES)
        w3 = (aligned("w3_dealt", [P, SLOTS, P, 2], U8), w23_scales[:, 0, :, :])
        w2 = (aligned("w2_dealt", [P, SLOTS, P, 2], U8), w23_scales[:, 1, :, :])
        nc.gpsimd.tensor_copy(w23_scales[:], w23_rows[:].rearrange("p i (m t) -> p i t m", t=SLOTS))
        nc.gpsimd.tensor_copy(w3[0][:], words_by_slot(w23_raw[:, 0, :]))
        nc.gpsimd.tensor_copy(w2[0][:], words_by_slot(w23_raw[:, 1, :]))

        shared = [(quarter, (t,)) for t in range(SLOTS) for quarter in range(2)]
        shared = shared + [(2, (0, 1, 2, 3)), (3, (0, 1)), (3, (2,)), (3, (3,))]
        member_tiles = {
            (quarter, slots): keep.tile([P, len(slots), S], F32, name="members%d_%d" % (quarter, slots[0]))
            for quarter, slots in shared
        }
        members = {(quarter, t): member_tiles[quarter, slots][:, i, :] for quarter, slots in shared for i, t in enumerate(slots)}
        gates_mid = keep.tile([P, SLOTS, QUARTER], F32, name="gates_mid")
        gates_last = keep.tile([P, SLOTS, QUARTER], F32, name="gates_last")
        z_left = keep.tile([P, SLOTS, HALF], BF16, name="z_left")
        z_mid = keep.tile([P, SLOTS, QUARTER], BF16, name="z_mid")
        z_last = keep.tile([P, SLOTS, QUARTER], BF16, name="z_last")

        def look_up(gather, quarter, t):
            gather(members[quarter, t], y[t], entries(n1_list, quarter * S, S))

        def sum_on_tensor(number, slots):
            sums = bank(number)
            pieces = [members[quarter, t] for t in slots for quarter in range(2)]
            for c, piece in enumerate(pieces):
                for d in range(MEMBERS):
                    nc.tensor.matmul(
                        sums[:, c * P : (c + 1) * P], lhsT=piece[:, d::MEMBERS], rhs=identity[:],
                        is_transpose=True, start=d == 0, stop=d == MEMBERS - 1,
                    )
            return sums[:, : len(pieces) * P]

        def gate_and_turn_back(number, sums, name):
            width = sums.shape[1]
            gates = bank(number)
            turned = aligned(name, [P, S], F32)
            nc.scalar.activation(turned[:, :width], sums, ACT.Sigmoid)
            for c in range(width // P):
                nc.tensor.transpose(gates[:, c * P : (c + 1) * P], turned[:, c * P : (c + 1) * P], identity[:])
            return gates

        def sum_on_vector(quarter, slots):
            width = len(slots) * QUARTER
            pairs = keep.tile([P, width, 2], F32, name="pairs%d_%d" % (quarter, slots[0]))
            sums = keep.tile([P, width], F32, name="sums%d_%d" % (quarter, slots[0]))
            fours = member_tiles[quarter, slots][:].rearrange("p t (j d) -> p (t j) d", d=MEMBERS)
            nc.vector.tensor_tensor(pairs[:], fours[:, :, 0:2], fours[:, :, 2:4], ALU.add)
            nc.vector.tensor_tensor(sums[:], pairs[:, :, 0], pairs[:, :, 1], ALU.add)
            return sums

        def gate(gates, slots, sums):
            nc.scalar.activation(gates[:, slots[0] : slots[-1] + 1, :].rearrange("p t j -> p (t j)"), sums[:], ACT.Sigmoid)

        def z_slot(z, t, gates, cols):
            nc.vector.scalar_tensor_tensor(z[:, t, :], gates, gain[:, t : t + 1], y[t][:, cols], ALU.mult, ALU.mult)

        def z_operand(name, grouped):
            width = grouped.shape[1]
            words, scales = aligned(name + "_words", [P, width], U32), aligned(name + "_scales", [P, width], U8)
            quantise(words[:], scales[:], grouped)
            return words[:], scales[:]

        def passes(banks, cols, weight, words, scales, start, stop):
            for t in H_ORDER:
                product(banks[t][:, cols], weight, t, words, scales, start, stop)

        left_pieces = [(quarter, t) for t in range(SLOTS) for quarter in range(2)]
        for quarter, t in left_pieces[:-1]:
            look_up(vector_gather, quarter, t)
        for t in range(SLOTS):
            look_up(scalar_gather, 2, t)
        sums01 = sum_on_tensor(0, (0, 1))
        sums2 = sum_on_tensor(2, (2,))
        gates01 = gate_and_turn_back(1, sums01, "turned01")
        look_up(scalar_gather, *left_pieces[-1])
        sums3 = sum_on_tensor(0, (3,))

        for t in (0, 1):
            look_up(scalar_gather, 3, t)
        sums_mid = sum_on_vector(2, (0, 1, 2, 3))
        for t in (0, 1):
            z_slot(z_left, t, gates01[:, t * HALF : (t + 1) * HALF], LEFT)
        x2_right = aligned("turned01", [P, HALF], U32)
        pick_words(x2_right[:], two_list, HALVES[1])
        gate(gates_mid, (0, 1, 2, 3), sums_mid)
        gates2 = gate_and_turn_back(3, sums2, "turned2")
        sums_last01 = sum_on_vector(3, (0, 1))
        gates3 = gate_and_turn_back(2, sums3, "turned3")
        for t in (2, 3):
            look_up(scalar_gather, 3, t)
        gate(gates_last, (0, 1), sums_last01)
        for t in range(SLOTS):
            z_slot(z_mid, t, gates_mid[:, t, :], MID)
        mid_grouped = group("z_mid", nc.vector.tensor_copy, z_mid[:])
        z_slot(z_left, 2, gates2[:, :HALF], LEFT)
        mid_operand = z_operand("z_mid", mid_grouped)
        z_slot(z_left, 3, gates3[:, :HALF], LEFT)

        h_early = {t: bank(number) for t, number in zip(H_ORDER, (1, 0, 3, 2))}
        h_late = [bank(SLOTS + t) for t in range(SLOTS)]
        late_cols = slice(0, QUARTER)
        passes(h_early, LEFT, w3, x2_left[:], x2_scales[:, LEFT], True, False)
        passes(h_early, MID, w3, x2_right[:, :QUARTER], x2_scales[:, MID], False, False)
        passes(h_late, late_cols, w3, x2_right[:, QUARTER:], x2_scales[:, LAST], True, False)
        passes(h_early, MID, w2, *mid_operand, False, False)
        left_grouped = group("z_left", nc.vector.tensor_copy, z_left[:])
        for t in (2, 3):
            gate(gates_last, (t,), sum_on_vector(3, (t,)))
        passes(h_early, LEFT, w2, *z_operand("z_left", left_grouped), False, True)
        for t in range(SLOTS):
            z_slot(z_last, t, gates_last[:, t, :], LAST)
        passes(h_late, late_cols, w2, *z_operand("z_last", group("z_last", nc.vector.tensor_copy, z_last[:])), False, True)

        for t in H_ORDER:
            nc.scalar.activation(h[t][:, : LAST.start], h_early[t][:, : LAST.start], ACT.Copy)
        for t in H_ORDER:
            if t < 2:
                nc.scalar.activation(h[t][:, LAST], h_late[t][:, late_cols], ACT.Copy)
            else:
                nc.vector.tensor_copy(h[t][:, LAST], h_late[t][:, late_cols])

        neg_su = [keep.tile([P, S], F32, name="neg_su%d" % t) for t in range(SLOTS)]

        def fetch_on_scalar(name, win, list_tile):
            fetched = keep.tile([P, S], F32, name=name)
            scalar_gather(fetched[:], win, list_tile[:])
            return fetched

        def fetch_on_vector(name, win, list_tile):
            fetched = keep.tile([P, S], F32, name=name)
            for cols in HALVES:
                vector_gather(fetched[:, cols], win, entries(list_tile, cols.start, HALF))
            return fetched

        def make_neg_st(t, fetched):
            nc.vector.tensor_tensor(neg_st[t][:, :S], fetched[:], h[t][:, :S], ALU.subtract)

        def make_neg_su(t, fetched):
            nc.vector.tensor_tensor(neg_su[t][:], fetched[:], neg_st[t][:, :S], ALU.min)

        by_n2 = {2: fetch_on_vector("by_n2_2", h[2], n2_list)}
        for t in (0, 1):
            by_n2[t] = fetch_on_scalar("by_n2_%d" % t, h[t], n2_list)
        make_neg_st(2, by_n2[2])
        by_n2[3] = fetch_on_vector("by_n2_3", h[3], n2_list)
        for t in (0, 1, 3):
            make_neg_st(t, by_n2[t])
        by_n3 = {t: fetch_on_scalar("by_n3_%d" % t, neg_st[t], n3_list) for t in (2, 0, 1)}
        make_neg_su(2, by_n3[2])
        by_n3[3] = fetch_on_vector("by_n3_3", neg_st[3], n3_list)
        for t in (0, 1, 3):
            make_neg_su(t, by_n3[t])

        result = keep.tile([P, SLOTS, S], F32, name="result")
        out_rows = out_0.rearrange("(p t) j -> p t j", t=SLOTS)

        def make_result(gather, t, cols):
            fetched = keep.tile([P, HALF], F32, name="by_n4_%d_%d" % (t, cols.start))
            gather(fetched[:], neg_su[t], entries(n4_list, cols.start, HALF))
            nc.vector.scalar_tensor_tensor(result[:, t, cols], fetched[:], -0.5, neg_su[t][:, cols], ALU.mult, ALU.subtract)

        def store_result(t):
            nc.sync.dma_start(out_rows[:, t, :], result[:, t, :])

        for t in (2, 0):
            for cols in HALVES:
                make_result(scalar_gather, t, cols)
            store_result(t)
        make_result(vector_gather, 3, HALVES[0])
        for cols in HALVES:
            make_result(scalar_gather, 1, cols)
        store_result(1)
        make_result(scalar_gather, 3, HALVES[1])
        store_result(3)

        out_words = out_1[0].rearrange("p n t -> p (n t)").bitcast(I32)
        out_scales = aligned("out_scales", [P, S], U8)
        first_grouped = group("out_first", nc.scalar.copy, result[:, :, HALVES[0]])
        second_grouped = group("out_second", nc.vector.tensor_copy, result[:, :, HALVES[1]])
        for name, cols, grouped in (("second", HALVES[1], second_grouped), ("first", HALVES[0], first_grouped)):
            words = aligned("out_words_" + name, [P, HALF], U32)
            quantise(words[:], out_scales[:, cols], grouped)
            nc.sync.dma_start(out_words[:, cols], words[:].bitcast(I32))
        for q in range(QUADRANTS):
            queue = nc.sync if q == QUADRANTS - 1 else nc.scalar
            queue.dma_start(out_2[0, 4 * q : 4 * q + 4, :].bitcast(I32), out_scales[scale_rows(q), :].bitcast(I32))
